import numpy as np
import ml_dtypes


def mxq(x, axis, fmt="e4m3"):
    dtype, down = {"e4m3": (ml_dtypes.float8_e4m3fn, 7), "e5m2": (ml_dtypes.float8_e5m2, 14)}[fmt]
    v = np.moveaxis(np.asarray(x, np.float32).astype(ml_dtypes.bfloat16).astype(np.float64), axis, -1)
    blocks = v.reshape(v.shape[:-1] + (-1, 32))
    amax = np.abs(blocks).max(-1, keepdims=True)
    byte = np.maximum(np.where(amax > 0, np.frexp(amax)[1] - 1 + 127, 0) - down, 1)
    scale = np.exp2(byte - 127.0)
    codes = (blocks / scale).astype(np.float32).astype(dtype).astype(np.float64)
    return np.moveaxis((codes * scale).reshape(v.shape), -1, axis)


WIDE = False


def mx_kscale(k):
    if not WIDE:
        return np.ones(k)
    levels = np.array([10, -10, 5, -5, 0])
    if k % 512:
        return np.exp2(np.random.permutation(np.resize(levels, k // 32))).repeat(32)
    a = np.empty((k // 512, 16))
    for p in range(k // 512):
        a[p, :8] = np.random.permutation(np.resize(levels, 8))
        for g in range(8):
            far = levels[np.abs(levels - a[p, g]) >= 10]
            a[p, g + 8] = far[np.random.randint(len(far))]
    return np.exp2(a.ravel()).repeat(32)


def f64(x):
    return np.asarray(x).astype(np.float64)


def striped(idx):
    return np.tile(np.asarray(idx).reshape(-1, 16).T, (8, 1)).astype(np.uint16)


def unstriped(offs):
    return offs[:16].T.reshape(-1).astype(np.int64)


E2M1 = np.array([0.0, 0.5, 1.0, 1.5, 2.0, 3.0, 4.0, 6.0, -0.0, -0.5, -1.0, -1.5, -2.0, -3.0, -4.0, -6.0])


def pack_weight(w, fmt):
    k, n = w.shape
    w = f64(np.asarray(w, np.float32).astype(ml_dtypes.bfloat16)).reshape(k // 32, 32, n)
    amax = np.abs(w).max(1)
    if fmt == "e4m3":
        byte = np.frexp(amax)[1] - 1 + 127 - 7
    else:
        mant, ex = np.frexp(amax / 6.0)
        byte = np.where(mant > 0.5, ex, ex - 1) + 127
    byte = np.clip(np.where(amax > 0, byte, 1), 1, 254)
    scaled = (w * np.exp2(127.0 - byte)[:, None, :]).reshape(k, n).astype(np.float32)
    by_word = np.ascontiguousarray(scaled.reshape(k // 512, 128, 4, n).transpose(0, 1, 3, 2))
    if fmt == "e4m3":
        words = by_word.astype(ml_dtypes.float8_e4m3fn).view(np.uint8)
    else:
        c = by_word.astype(ml_dtypes.float4_e2m1fn).view(np.uint8) & 0xF
        words = (c[..., 0::2] | (c[..., 1::2] << 4)).reshape(k // 512, 128, 2 * n)
    return np.ascontiguousarray(words), np.ascontiguousarray(byte.astype(np.uint8).reshape(k // 512, 16, n))


def unpack_weight(words, scales, fmt):
    g, _, n = scales.shape
    words = np.ascontiguousarray(words).reshape(g, 128, n, -1)
    if fmt == "e4m3":
        vals = words.view(ml_dtypes.float8_e4m3fn).astype(np.float64)
    else:
        nib = np.empty((g, 128, n, 4), np.uint8)
        nib[..., 0::2] = words & 0xF
        nib[..., 1::2] = words >> 4
        vals = E2M1[nib]
    vals = vals * np.repeat(np.exp2(scales.astype(np.float64) - 127.0), 8, axis=1)[..., None]
    return vals.transpose(0, 1, 3, 2).reshape(g * 512, n)


D, E, T, I, Q = 512, 512, 2048, 512, 128


def setup_inputs():
    n = np.random.standard_normal
    idx = np.random.permutation(T)[:I]
    fd = mx_kscale(D)
    fe = mx_kscale(E)
    keysp = pack_weight(n((D, T)) / fd[:, None], "e2m1")
    valsp = pack_weight(n((E, T)) / fe[:, None], "e2m1")
    return {
        "query": (n((D, Q)) * 0.8 / np.sqrt(D) * fd[:, None]).astype(np.float32),
        "keys_words": keysp[0],
        "keys_scales": keysp[1],
        "bonus": (np.random.uniform(0.5, 2.0, (Q, 1))).astype(np.float32),
        "gout": (n((E, Q)) * 1 / np.sqrt(E) * fe[:, None]).astype(np.float32),
        "vals_words": valsp[0],
        "vals_scales": valsp[1],
        "dquery": (n((D, Q)) * 1.0 / np.sqrt(D) * fd[:, None]).astype(np.float32),
        "base": (0.5 * n((Q, T))).astype(np.float32),
        "offs": striped(idx),
    }


def reference(query, keys_words, keys_scales, bonus, gout, vals_words, vals_scales, dquery, base, offs):
    idx = unstriped(offs)
    keysu = unpack_weight(keys_words, keys_scales, "e2m1")
    valsu = unpack_weight(vals_words, vals_scales, "e2m1")
    queryq = mxq(f64(query), 0, "e4m3")
    keysidxg = keysu[:, idx]
    a = queryq.T @ keysidxg
    dqueryq = mxq(f64(dquery), 0, "e4m3")
    ta = dqueryq.T @ keysidxg
    b = a - np.max(a, axis=1, keepdims=True)
    p = np.exp(b)
    z = np.sum(p, axis=1, keepdims=True)
    goutq = mxq(f64(gout), 0, "e4m3")
    valsidxg = valsu[:, idx]
    c0 = goutq.T @ valsidxg
    dz = f64(bonus) / z - np.sum(p * c0, axis=1, keepdims=True) / np.square(z) - f64(bonus) * (-1.0) * np.sum(p * b, axis=1, keepdims=True) / np.square(z)
    dp = 1.0 / z * c0 + f64(bonus) * (-1.0) / z * b + dz
    tb = ta
    tp = tb * p
    tz = np.sum(tp, axis=1, keepdims=True)
    tdz = tz * f64(bonus) / np.square(z) * (-1.0) - (np.sum(tp * c0, axis=1, keepdims=True) - tz * z * 2.0 * np.sum(p * c0, axis=1, keepdims=True) / np.square(z)) / np.square(z) - (np.sum(tp * b + tb * p, axis=1, keepdims=True) * f64(bonus) * (-1.0) - tz * z * 2.0 * f64(bonus) * (-1.0) * np.sum(p * b, axis=1, keepdims=True) / np.square(z)) / np.square(z)
    tdp = tz * 1.0 / np.square(z) * (-1.0) * c0 + tz * f64(bonus) * (-1.0) / np.square(z) * (-1.0) * b + tb * f64(bonus) * (-1.0) / z + tdz
    tdb = tz * f64(bonus) * (-1.0) / np.square(z) * (-1.0) * p + tp * f64(bonus) * (-1.0) / z + tdp * p + tp * dp
    gs = tdb * 512.0
    gf = np.zeros((Q, T))
    gf[:, idx] = gs
    y = f64(base) + gf
    return y

@@ -1,0 +1,170 @@
+from contextlib import ExitStack
+
+import concourse.mybir as mybir
+
+D, T, I, Q = 512, 2048, 512, 128
+FLOPS = 3 * 2 * D * Q * I
+
+F32 = mybir.dt.float32
+BF16 = mybir.dt.bfloat16
+I32 = mybir.dt.int32
+U32 = mybir.dt.uint32
+U16 = mybir.dt.uint16
+U8 = mybir.dt.uint8
+FP8X4 = mybir.dt.float8_e4m3fn_x4
+FP4X4 = mybir.dt.float4_e2m1fn_x4
+ALU = mybir.AluOpType
+ACT = mybir.ActivationFunctionType
+
+P = 128
+PACK = 4
+OUT_CHUNKS = (256, 512, 512, 512, 256)
+
+
+def tile_attend_hventropybonus_s_kernel(
+    tc, query, keys_words, keys_scales, bonus, gout, vals_words, vals_scales, dquery, base, offs, out
+):
+    nc = tc.nc
+    with ExitStack() as ctx:
+        sb = ctx.enter_context(tc.tile_pool(name="sb", bufs=1))
+        psum = ctx.enter_context(tc.psum_pool(name="psum", bufs=1))
+
+        def load_words(name, words):
+            pool_words = sb.tile([P, T], U16, name=name)
+            nc.sync.dma_start(out=pool_words[:].bitcast(I32), in_=words[0].bitcast(I32))
+            return pool_words
+
+        def load_scales(name, scales, queue):
+            pool_scales = sb.tile([P, T], U8, name=name)
+            nc.vector.memset(pool_scales[:].bitcast(I32), 0)
+            for quad in range(4):
+                queue.dma_start(
+                    out=pool_scales[32 * quad : 32 * quad + 4, :].bitcast(I32),
+                    in_=scales[0, 4 * quad : 4 * quad + 4, :].bitcast(I32),
+                )
+            return pool_scales
+
+        def load_rows(name, x):
+            raw = sb.tile([P, PACK, Q], F32, name=name)
+            nc.sync.dma_start(out=raw[:], in_=x.rearrange("(p j) q -> p j q", j=PACK))
+            return raw
+
+        def interleave(name, raw):
+            grouped = sb.tile([P, Q, PACK], BF16, name=name, align_bytes=64)
+            nc.scalar.copy(
+                out=grouped[:].rearrange("p (c i) j -> p c j i", i=4),
+                in_=raw[:].rearrange("p j (c i) -> p c j i", i=4),
+            )
+            return grouped
+
+        def quantize(name, grouped):
+            codes = sb.tile([P, Q], U32, name=name + "_codes", align_bytes=64)
+            scales = sb.tile([P, Q], U8, name=name + "_scales", align_bytes=64)
+            nc.vector.quantize_mx(
+                out=codes[:].bitcast(FP8X4), scales=scales[:], in_=grouped[:].rearrange("p q j -> p (q j)")
+            )
+            return codes, scales
+
+        def gather(name, window, dtype):
+            listed = sb.tile([P, I], dtype, name=name, align_bytes=64)
+            nc.vector.tensor_copy(listed[:], window[:].indirect(offsets[:]))
+            return listed
+
+        def product(name, rows, words, scales):
+            acc = psum.tile([Q, I], F32, name=name)
+            nc.tensor.matmul_mx(
+                out=acc[:],
+                lhsT=rows[0][:].bitcast(FP8X4),
+                lhsT_scale=rows[1][:],
+                rhs=words[:].bitcast(FP4X4),
+                rhs_scale=scales[:],
+                start=True,
+                stop=True,
+            )
+            return acc
+
+        offsets = sb.tile([P, I // 16], U16, name="offsets")
+        nc.sync.dma_start(offsets[:], offs)
+        key_words = load_words("key_words", keys_words)
+        val_words = load_words("val_words", vals_words)
+        query_raw = load_rows("query_raw", query)
+        key_scales = load_scales("key_scales", keys_scales, nc.scalar)
+        gout_raw = load_rows("gout_raw", gout)
+        dquery_raw = load_rows("dquery_raw", dquery)
+        val_scales = load_scales("val_scales", vals_scales, nc.sync)
+        beta = sb.tile([P, 1], F32, name="beta")
+        nc.gpsimd.dma_start(out=beta[:], in_=bonus)
+
+        placed = sb.tile([P, T], F32, name="placed")
+        nc.vector.memset(placed[:], 0.0)
+
+        query_bf = interleave("query_bf", query_raw)
+        gout_bf = interleave("gout_bf", gout_raw)
+        dquery_bf = interleave("dquery_bf", dquery_raw)
+
+        kw = gather("kw", key_words, U16)
+        vw = gather("vw", val_words, U16)
+        ks = gather("ks", key_scales, U8)
+        query_mx = quantize("query", query_bf)
+        a = product("a", query_mx, kw, ks)
+        gout_mx = quantize("gout", gout_bf)
+        dquery_mx = quantize("dquery", dquery_bf)
+        ta = product("ta", dquery_mx, kw, ks)
+
+        neg_a = sb.tile([P, I], F32, name="neg_a")
+        neg_max = sb.tile([P, 1], F32, name="neg_max")
+        nc.vector.tensor_scalar(
+            out=neg_a[:], in0=a[:], scalar1=-1.0, scalar2=None, op0=ALU.mult, op1=ALU.min, accum_out=neg_max[:]
+        )
+        p = sb.tile([P, I], F32, name="p")
+        z = sb.tile([P, 1], F32, name="z", tag="u")
+        nc.scalar.activation(out=p[:], in_=neg_a[:], func=ACT.Exp, bias=neg_max[:], scale=-1.0, accum_out=z[:])
+        vs = gather("vs", val_scales, U8)
+        c0 = product("c0", gout_mx, vw, vs)
+        base_sb = sb.tile([P, T], F32, name="base_sb", tag="val_scales")
+        nc.sync.dma_start(out=base_sb[:], in_=base)
+
+        inv_z = sb.tile([P, 1], F32, name="inv_z")
+        nc.vector.reciprocal(inv_z[:], z[:])
+        w = sb.tile([P, I], F32, name="w")
+        nc.scalar.activation(out=w[:], in_=p[:], func=ACT.Copy, scale=inv_z[:])
+        w_out = sb.tile([P, I], F32, name="w_out")
+        nc.scalar.activation(out=w_out[:], in_=w[:], func=ACT.Copy, scale=512.0)
+
+        w_ta = sb.tile([P, I], F32, name="w_ta")
+        mean_ta = sb.tile([P, 1], F32, name="mean_ta")
+        nc.vector.scalar_tensor_tensor(
+            out=w_ta[:], in0=ta[:], scalar=inv_z[:], in1=p[:], op0=ALU.mult, op1=ALU.mult, accum_out=mean_ta[:]
+        )
+        u = sb.tile([P, I], F32, name="u")
+        nc.vector.scalar_tensor_tensor(
+            out=u[:], in0=neg_a[:], scalar=beta[:], in1=c0[:], op0=ALU.mult, op1=ALU.add
+        )
+        wd = sb.tile([P, I], F32, name="wd")
+        nc.vector.scalar_tensor_tensor(
+            out=wd[:], in0=ta[:], scalar=mean_ta[:], in1=w_out[:], op0=ALU.subtract, op1=ALU.mult
+        )
+        w_u = sb.tile([P, I], F32, name="w_u")
+        shift = sb.tile([P, 1], F32, name="shift")
+        nc.vector.scalar_tensor_tensor(
+            out=w_u[:], in0=u[:], scalar=beta[:], in1=w[:], op0=ALU.add, op1=ALU.mult, accum_out=shift[:]
+        )
+        x = sb.tile([P, I], F32, name="x")
+        cov = sb.tile([P, 1], F32, name="cov")
+        nc.vector.scalar_tensor_tensor(
+            out=x[:], in0=u[:], scalar=shift[:], in1=wd[:], op0=ALU.subtract, op1=ALU.mult, accum_out=cov[:]
+        )
+        y = sb.tile([P, I], F32, name="y")
+        nc.vector.tensor_scalar(
+            out=y[:], in0=w[:], scalar1=cov[:], scalar2=-1.0, op0=ALU.mult, op1=ALU.mult
+        )
+        nc.vector.tensor_tensor(placed[:].indirect(offsets[:]), x[:], y[:], ALU.add)
+
+        start = 0
+        for n, width in enumerate(OUT_CHUNKS):
+            cols = slice(start, start + width)
+            res = sb.tile([P, width], F32, name="res%d" % n)
+            nc.vector.tensor_tensor(res[:], placed[:, cols], base_sb[:, cols], ALU.add)
+            queue = nc.sync if n % 2 == 0 else nc.scalar
+            queue.dma_start(out=out[:, cols], in_=res[:])
+            start = start + width

@@ -44,9 +44,9 @@ def tile_attend_hventropybonus_s_kernel(
                 )
             return pool_scales
 
-        def load_rows(name, x):
-            raw = sb.tile([P, PACK, Q], F32, name=name)
-            nc.sync.dma_start(out=raw[:], in_=x.rearrange("(p j) q -> p j q", j=PACK))
+        def load_rows(name, x, queue, tag):
+            raw = sb.tile([P, PACK, Q], F32, name=name, tag=tag, align_bytes=64)
+            queue.dma_start(out=raw[:], in_=x.rearrange("(p j) q -> p j q", j=PACK))
             return raw
 
         def interleave(name, raw):
@@ -65,8 +65,8 @@ def tile_attend_hventropybonus_s_kernel(
             )
             return codes, scales
 
-        def gather(name, window, dtype):
-            listed = sb.tile([P, I], dtype, name=name, align_bytes=64)
+        def gather(name, window, dtype, tag):
+            listed = sb.tile([P, I], dtype, name=name, tag=tag, align_bytes=64)
             nc.vector.tensor_copy(listed[:], window[:].indirect(offsets[:]))
             return listed
 
@@ -86,43 +86,43 @@ def tile_attend_hventropybonus_s_kernel(
         offsets = sb.tile([P, I // 16], U16, name="offsets")
         nc.sync.dma_start(offsets[:], offs)
         key_words = load_words("key_words", keys_words)
+        key_scales = load_scales("key_scales", keys_scales, nc.sync)
+        query_raw = load_rows("query_raw", query, nc.sync, "query_raw")
         val_words = load_words("val_words", vals_words)
-        query_raw = load_rows("query_raw", query)
-        key_scales = load_scales("key_scales", keys_scales, nc.scalar)
-        gout_raw = load_rows("gout_raw", gout)
-        dquery_raw = load_rows("dquery_raw", dquery)
+        dquery_raw = load_rows("dquery_raw", dquery, nc.sync, "dquery_raw")
         val_scales = load_scales("val_scales", vals_scales, nc.sync)
+        gout_raw = load_rows("gout_raw", gout, nc.sync, "gout_raw")
         beta = sb.tile([P, 1], F32, name="beta")
-        nc.gpsimd.dma_start(out=beta[:], in_=bonus)
+        nc.sync.dma_start(out=beta[:], in_=bonus)
+        base_sb = sb.tile([P, T], F32, name="base_sb")
+        nc.sync.dma_start(out=base_sb[:], in_=base)
 
         placed = sb.tile([P, T], F32, name="placed")
         nc.vector.memset(placed[:], 0.0)
 
         query_bf = interleave("query_bf", query_raw)
-        gout_bf = interleave("gout_bf", gout_raw)
         dquery_bf = interleave("dquery_bf", dquery_raw)
+        gout_bf = interleave("gout_bf", gout_raw)
 
-        kw = gather("kw", key_words, U16)
-        vw = gather("vw", val_words, U16)
-        ks = gather("ks", key_scales, U8)
+        kw = gather("kw", key_words, U16, "kw")
+        ks = gather("ks", key_scales, U8, "ks")
         query_mx = quantize("query", query_bf)
         a = product("a", query_mx, kw, ks)
-        gout_mx = quantize("gout", gout_bf)
-        dquery_mx = quantize("dquery", dquery_bf)
-        ta = product("ta", dquery_mx, kw, ks)
+        vw = gather("vw", val_words, U16, "query_raw")
 
         neg_a = sb.tile([P, I], F32, name="neg_a")
         neg_max = sb.tile([P, 1], F32, name="neg_max")
         nc.vector.tensor_scalar(
             out=neg_a[:], in0=a[:], scalar1=-1.0, scalar2=None, op0=ALU.mult, op1=ALU.min, accum_out=neg_max[:]
         )
-        p = sb.tile([P, I], F32, name="p")
+        p = sb.tile([P, I], F32, name="p", tag="gout_raw", align_bytes=64)
         z = sb.tile([P, 1], F32, name="z", tag="u")
         nc.scalar.activation(out=p[:], in_=neg_a[:], func=ACT.Exp, bias=neg_max[:], scale=-1.0, accum_out=z[:])
-        vs = gather("vs", val_scales, U8)
+        dquery_mx = quantize("dquery", dquery_bf)
+        ta = product("ta", dquery_mx, kw, ks)
+        vs = gather("vs", val_scales, U8, "dquery_raw")
+        gout_mx = quantize("gout", gout_bf)
         c0 = product("c0", gout_mx, vw, vs)
-        base_sb = sb.tile([P, T], F32, name="base_sb", tag="val_scales")
-        nc.sync.dma_start(out=base_sb[:], in_=base)
 
         inv_z = sb.tile([P, 1], F32, name="inv_z")
         nc.vector.reciprocal(inv_z[:], z[:])

from contextlib import ExitStack

import concourse.mybir as mybir

D, T, I, Q = 512, 2048, 512, 128
FLOPS = 3 * 2 * D * Q * I

F32 = mybir.dt.float32
BF16 = mybir.dt.bfloat16
I32 = mybir.dt.int32
U32 = mybir.dt.uint32
U16 = mybir.dt.uint16
U8 = mybir.dt.uint8
FP8X4 = mybir.dt.float8_e4m3fn_x4
FP4X4 = mybir.dt.float4_e2m1fn_x4
ALU = mybir.AluOpType
ACT = mybir.ActivationFunctionType

P = 128
PACK = 4
OUT_CHUNKS = (256, 512, 512, 512, 256)


def tile_attend_hventropybonus_s_kernel(
    tc, query, keys_words, keys_scales, bonus, gout, vals_words, vals_scales, dquery, base, offs, out
):
    nc = tc.nc
    with ExitStack() as ctx:
        sb = ctx.enter_context(tc.tile_pool(name="sb", bufs=1))
        psum = ctx.enter_context(tc.psum_pool(name="psum", bufs=1))

        def load_words(name, words):
            pool_words = sb.tile([P, T], U16, name=name)
            nc.sync.dma_start(out=pool_words[:].bitcast(I32), in_=words[0].bitcast(I32))
            return pool_words

        def load_scales(name, scales, queue):
            pool_scales = sb.tile([P, T], U8, name=name)
            nc.vector.memset(pool_scales[:].bitcast(I32), 0)
            for quad in range(4):
                queue.dma_start(
                    out=pool_scales[32 * quad : 32 * quad + 4, :].bitcast(I32),
                    in_=scales[0, 4 * quad : 4 * quad + 4, :].bitcast(I32),
                )
            return pool_scales

        def load_rows(name, x, queue, tag):
            raw = sb.tile([P, PACK, Q], F32, name=name, tag=tag, align_bytes=64)
            queue.dma_start(out=raw[:], in_=x.rearrange("(p j) q -> p j q", j=PACK))
            return raw

        def interleave(name, raw):
            grouped = sb.tile([P, Q, PACK], BF16, name=name, align_bytes=64)
            nc.scalar.copy(
                out=grouped[:].rearrange("p (c i) j -> p c j i", i=4),
                in_=raw[:].rearrange("p j (c i) -> p c j i", i=4),
            )
            return grouped

        def quantize(name, grouped):
            codes = sb.tile([P, Q], U32, name=name + "_codes", align_bytes=64)
            scales = sb.tile([P, Q], U8, name=name + "_scales", align_bytes=64)
            nc.vector.quantize_mx(
                out=codes[:].bitcast(FP8X4), scales=scales[:], in_=grouped[:].rearrange("p q j -> p (q j)")
            )
            return codes, scales

        def gather(name, window, dtype, tag):
            listed = sb.tile([P, I], dtype, name=name, tag=tag, align_bytes=64)
            nc.vector.tensor_copy(listed[:], window[:].indirect(offsets[:]))
            return listed

        def product(name, rows, words, scales):
            acc = psum.tile([Q, I], F32, name=name)
            nc.tensor.matmul_mx(
                out=acc[:],
                lhsT=rows[0][:].bitcast(FP8X4),
                lhsT_scale=rows[1][:],
                rhs=words[:].bitcast(FP4X4),
                rhs_scale=scales[:],
                start=True,
                stop=True,
            )
            return acc

        offsets = sb.tile([P, I // 16], U16, name="offsets")
        nc.sync.dma_start(offsets[:], offs)
        key_words = load_words("key_words", keys_words)
        key_scales = load_scales("key_scales", keys_scales, nc.sync)
        query_raw = load_rows("query_raw", query, nc.sync, "query_raw")
        val_words = load_words("val_words", vals_words)
        dquery_raw = load_rows("dquery_raw", dquery, nc.sync, "dquery_raw")
        val_scales = load_scales("val_scales", vals_scales, nc.sync)
        gout_raw = load_rows("gout_raw", gout, nc.sync, "gout_raw")
        beta = sb.tile([P, 1], F32, name="beta")
        nc.sync.dma_start(out=beta[:], in_=bonus)
        base_sb = sb.tile([P, T], F32, name="base_sb")
        nc.sync.dma_start(out=base_sb[:], in_=base)

        placed = sb.tile([P, T], F32, name="placed")
        nc.vector.memset(placed[:], 0.0)

        query_bf = interleave("query_bf", query_raw)
        dquery_bf = interleave("dquery_bf", dquery_raw)
        gout_bf = interleave("gout_bf", gout_raw)

        kw = gather("kw", key_words, U16, "kw")
        ks = gather("ks", key_scales, U8, "ks")
        query_mx = quantize("query", query_bf)
        a = product("a", query_mx, kw, ks)
        vw = gather("vw", val_words, U16, "query_raw")

        neg_a = sb.tile([P, I], F32, name="neg_a")
        neg_max = sb.tile([P, 1], F32, name="neg_max")
        nc.vector.tensor_scalar(
            out=neg_a[:], in0=a[:], scalar1=-1.0, scalar2=None, op0=ALU.mult, op1=ALU.min, accum_out=neg_max[:]
        )
        p = sb.tile([P, I], F32, name="p", tag="gout_raw", align_bytes=64)
        z = sb.tile([P, 1], F32, name="z", tag="u")
        nc.scalar.activation(out=p[:], in_=neg_a[:], func=ACT.Exp, bias=neg_max[:], scale=-1.0, accum_out=z[:])
        dquery_mx = quantize("dquery", dquery_bf)
        ta = product("ta", dquery_mx, kw, ks)
        vs = gather("vs", val_scales, U8, "dquery_raw")
        gout_mx = quantize("gout", gout_bf)
        c0 = product("c0", gout_mx, vw, vs)

        inv_z = sb.tile([P, 1], F32, name="inv_z")
        nc.vector.reciprocal(inv_z[:], z[:])
        w = sb.tile([P, I], F32, name="w")
        nc.scalar.activation(out=w[:], in_=p[:], func=ACT.Copy, scale=inv_z[:])
        w_out = sb.tile([P, I], F32, name="w_out")
        nc.scalar.activation(out=w_out[:], in_=w[:], func=ACT.Copy, scale=512.0)

        w_ta = sb.tile([P, I], F32, name="w_ta")
        mean_ta = sb.tile([P, 1], F32, name="mean_ta")
        nc.vector.scalar_tensor_tensor(
            out=w_ta[:], in0=ta[:], scalar=inv_z[:], in1=p[:], op0=ALU.mult, op1=ALU.mult, accum_out=mean_ta[:]
        )
        u = sb.tile([P, I], F32, name="u")
        nc.vector.scalar_tensor_tensor(
            out=u[:], in0=neg_a[:], scalar=beta[:], in1=c0[:], op0=ALU.mult, op1=ALU.add
        )
        wd = sb.tile([P, I], F32, name="wd")
        nc.vector.scalar_tensor_tensor(
            out=wd[:], in0=ta[:], scalar=mean_ta[:], in1=w_out[:], op0=ALU.subtract, op1=ALU.mult
        )
        w_u = sb.tile([P, I], F32, name="w_u")
        shift = sb.tile([P, 1], F32, name="shift")
        nc.vector.scalar_tensor_tensor(
            out=w_u[:], in0=u[:], scalar=beta[:], in1=w[:], op0=ALU.add, op1=ALU.mult, accum_out=shift[:]
        )
        x = sb.tile([P, I], F32, name="x")
        cov = sb.tile([P, 1], F32, name="cov")
        nc.vector.scalar_tensor_tensor(
            out=x[:], in0=u[:], scalar=shift[:], in1=wd[:], op0=ALU.subtract, op1=ALU.mult, accum_out=cov[:]
        )
        y = sb.tile([P, I], F32, name="y")
        nc.vector.tensor_scalar(
            out=y[:], in0=w[:], scalar1=cov[:], scalar2=-1.0, op0=ALU.mult, op1=ALU.mult
        )
        nc.vector.tensor_tensor(placed[:].indirect(offsets[:]), x[:], y[:], ALU.add)

        start = 0
        for n, width in enumerate(OUT_CHUNKS):
            cols = slice(start, start + width)
            res = sb.tile([P, width], F32, name="res%d" % n)
            nc.vector.tensor_tensor(res[:], placed[:, cols], base_sb[:, cols], ALU.add)
            queue = nc.sync if n % 2 == 0 else nc.scalar
            queue.dma_start(out=out[:, cols], in_=res[:])
            start = start + width
